import numpy as np
import ml_dtypes


def mxq(x, axis, fmt="e4m3"):
    dtype, down = {"e4m3": (ml_dtypes.float8_e4m3fn, 7), "e5m2": (ml_dtypes.float8_e5m2, 14)}[fmt]
    v = np.moveaxis(np.asarray(x, np.float32).astype(ml_dtypes.bfloat16).astype(np.float64), axis, -1)
    blocks = v.reshape(v.shape[:-1] + (-1, 32))
    amax = np.abs(blocks).max(-1, keepdims=True)
    byte = np.maximum(np.where(amax > 0, np.frexp(amax)[1] - 1 + 127, 0) - down, 1)
    scale = np.exp2(byte - 127.0)
    codes = (blocks / scale).astype(np.float32).astype(dtype).astype(np.float64)
    return np.moveaxis((codes * scale).reshape(v.shape), -1, axis)


WIDE = False


def mx_kscale(k):
    if not WIDE:
        return np.ones(k)
    levels = np.array([10, -10, 5, -5, 0])
    if k % 512:
        return np.exp2(np.random.permutation(np.resize(levels, k // 32))).repeat(32)
    a = np.empty((k // 512, 16))
    for p in range(k // 512):
        a[p, :8] = np.random.permutation(np.resize(levels, 8))
        for g in range(8):
            far = levels[np.abs(levels - a[p, g]) >= 10]
            a[p, g + 8] = far[np.random.randint(len(far))]
    return np.exp2(a.ravel()).repeat(32)


def f64(x):
    return np.asarray(x).astype(np.float64)


E2M1 = np.array([0.0, 0.5, 1.0, 1.5, 2.0, 3.0, 4.0, 6.0, -0.0, -0.5, -1.0, -1.5, -2.0, -3.0, -4.0, -6.0])


def pack_weight(w, fmt):
    k, n = w.shape
    w = f64(np.asarray(w, np.float32).astype(ml_dtypes.bfloat16)).reshape(k // 32, 32, n)
    amax = np.abs(w).max(1)
    if fmt == "e4m3":
        byte = np.frexp(amax)[1] - 1 + 127 - 7
    else:
        mant, ex = np.frexp(amax / 6.0)
        byte = np.where(mant > 0.5, ex, ex - 1) + 127
    byte = np.clip(np.where(amax > 0, byte, 1), 1, 254)
    scaled = (w * np.exp2(127.0 - byte)[:, None, :]).reshape(k, n).astype(np.float32)
    by_word = np.ascontiguousarray(scaled.reshape(k // 512, 128, 4, n).transpose(0, 1, 3, 2))
    if fmt == "e4m3":
        words = by_word.astype(ml_dtypes.float8_e4m3fn).view(np.uint8)
    else:
        c = by_word.astype(ml_dtypes.float4_e2m1fn).view(np.uint8) & 0xF
        words = (c[..., 0::2] | (c[..., 1::2] << 4)).reshape(k // 512, 128, 2 * n)
    return np.ascontiguousarray(words), np.ascontiguousarray(byte.astype(np.uint8).reshape(k // 512, 16, n))


def unpack_weight(words, scales, fmt):
    g, _, n = scales.shape
    words = np.ascontiguousarray(words).reshape(g, 128, n, -1)
    if fmt == "e4m3":
        vals = words.view(ml_dtypes.float8_e4m3fn).astype(np.float64)
    else:
        nib = np.empty((g, 128, n, 4), np.uint8)
        nib[..., 0::2] = words & 0xF
        nib[..., 1::2] = words >> 4
        vals = E2M1[nib]
    vals = vals * np.repeat(np.exp2(scales.astype(np.float64) - 127.0), 8, axis=1)[..., None]
    return vals.transpose(0, 1, 3, 2).reshape(g * 512, n)


def bf(x):
    return np.asarray(x, np.float32).astype(ml_dtypes.bfloat16)


def planes(Y):
    r, m = Y.shape
    b = f64(bf(Y)).reshape(r // 32, 32, m)
    amax = np.abs(b).max(1)
    byte = np.clip(np.where(amax > 0, np.frexp(amax)[1] - 1 + 127 - 7, 1), 1, 254)
    codes = (b * np.exp2(127.0 - byte)[:, None, :]).reshape(r, m).astype(np.float32).astype(ml_dtypes.float8_e4m3fn).view(np.uint8)
    words = codes.reshape(r // 512, 128, 4, m).transpose(0, 1, 3, 2)
    return np.ascontiguousarray(words), np.ascontiguousarray(byte.astype(np.uint8).reshape(r // 512, 16, m))


K, L, T, I, N = 1024, 512, 1024, 512, 512


def setup_inputs():
    n = np.random.standard_normal
    fk = mx_kscale(K)
    fl = mx_kscale(L)
    wap = pack_weight(n((K, N)) * 1 / np.sqrt(K) * fk[:, None], "e4m3")
    wbp = pack_weight(n((K, N)) * 1 / np.sqrt(K) * fk[:, None], "e2m1")
    xqp = pack_weight(n((L, I)) / fl[:, None], "e4m3")
    wqp = pack_weight(n((L, N)) * 1 / np.sqrt(L) * fl[:, None], "e2m1")
    return {
        "xf": (n((K, T)) / fk[:, None]).astype(np.float32),
        "wa_words": wap[0],
        "wa_scales": wap[1],
        "wb_words": wbp[0],
        "wb_scales": wbp[1],
        "xq_words": xqp[0],
        "xq_scales": xqp[1],
        "wq_words": wqp[0],
        "wq_scales": wqp[1],
        "b": (np.random.uniform(-0.5, 0.5, (N, 1))).astype(np.float32),
    }


def reference(xf, wa_words, wa_scales, wb_words, wb_scales, xq_words, xq_scales, wq_words, wq_scales, b):
    wau = unpack_weight(wa_words, wa_scales, "e4m3")
    wbu = unpack_weight(wb_words, wb_scales, "e2m1")
    xqu = unpack_weight(xq_words, xq_scales, "e4m3")
    wqu = unpack_weight(wq_words, wq_scales, "e2m1")
    xa = f64(xf)[:, 0:0 + I]
    xb = f64(xf)[:, 512:512 + I]
    xaq = mxq(xa, 0, "e4m3")
    xbq = mxq(xb, 0, "e4m3")
    z = wau.T @ xaq + wbu.T @ xbq + wqu.T @ xqu
    y = np.tanh(0.5 * z + f64(b))
    words, scales = planes(y)
    return y, words, scales

@@ -1,0 +1,236 @@
+from contextlib import ExitStack
+
+import concourse.mybir as mybir
+
+K, L, T, I, N = 1024, 512, 1024, 512, 512
+FLOPS = 2 * N * I * (2 * K + L)
+
+F32 = mybir.dt.float32
+BF16 = mybir.dt.bfloat16
+I32 = mybir.dt.int32
+U32 = mybir.dt.uint32
+U8 = mybir.dt.uint8
+FP8X4 = mybir.dt.float8_e4m3fn_x4
+FP4X4 = mybir.dt.float4_e2m1fn_x4
+ACT = mybir.ActivationFunctionType
+
+P = 128
+PACK = 4
+W = 128
+CHUNKS = I // W
+LAST = CHUNKS - 1
+LINE = 16
+STORES = [(0, 2), (2, 1), (3, 1)]
+
+
+def deal(nc, dst, src, elems, elem_bytes):
+    run = LINE // (elems * elem_bytes)
+    nc.vector.tensor_copy(
+        out=dst.rearrange("p (r c i e) -> p c r i e", r=PACK, i=run, e=elems),
+        in_=src.rearrange("p (c i r e) -> p c r i e", r=PACK, i=run, e=elems),
+    )
+
+
+def load_scale_rows(queue, plane, first, scales):
+    passes = scales.shape[0]
+    for q in range(4):
+        rows = slice(32 * q + first, 32 * q + first + 4)
+        queue.dma_start(
+            out=plane[rows, :].bitcast(I32).rearrange("r (z c) -> r z c", z=passes),
+            in_=scales[:, 4 * q : 4 * q + 4, :].rearrange("z r c -> r z c").bitcast(I32),
+        )
+
+
+def tile_mix_halves_in_one_sum_pl_kernel(
+    tc, xf, wa_words, wa_scales, wb_words, wb_scales, xq_words, xq_scales, wq_words, wq_scales, b, out_0, out_1, out_2
+):
+    nc = tc.nc
+    with ExitStack() as ctx:
+        sb = ctx.enter_context(tc.tile_pool(name="sb", bufs=1))
+        ps = ctx.enter_context(tc.psum_pool(name="ps", bufs=1))
+        ctx.enter_context(tc.manual_schedule())
+
+        def tile(name, cols, dtype):
+            return sb.tile([P, cols], dtype, name=name, align_bytes=64)
+
+        wa_raw, wa = tile("wa_raw", 2 * N, U32), tile("wa", 2 * N, U32)
+        wb_raw, wb = tile("wb_raw", 4 * N, U8), tile("wb", 4 * N, U8)
+        wq_raw, wq = tile("wq_raw", 2 * N, U8), tile("wq", 2 * N, U8)
+        sab_raw, sab = tile("sab_raw", 2 * N, U8), tile("sab", 2 * N, U8)
+        sq_raw, sq = tile("sq_raw", N, U8), tile("sq", N, U8)
+        xq = tile("xq", I, U32)
+        xq_plane = tile("xq_plane", I, U8)
+        bias = tile("bias", PACK, F32)
+        y = sb.tile([P, PACK, I], F32, name="y", align_bytes=64)
+        y_codes = tile("y_codes", I, U32)
+        y_plane = tile("y_plane", I, U8)
+
+        x_rows = xf.rearrange("(z p j) t -> z p (j t)", p=P, j=PACK).rearrange("z p (g i) -> z p g i", i=I)
+        raw = {}
+
+        def load_x(c, z):
+            cols = slice(c * W, (c + 1) * W)
+            if (c, z) == (LAST, 1):
+                for h in range(2):
+                    t = sb.tile([P, PACK, W], F32, name="x_raw_last%d" % h, align_bytes=64)
+                    nc.sync.dma_start(out=t[:], in_=x_rows[z, :, h::2, cols])
+                    raw[c, z, h] = t[:]
+            else:
+                t = sb.tile([P, 2 * PACK, W], F32, name="x_raw%d_%d" % (c, z), align_bytes=64)
+                nc.sync.dma_start(out=t[:], in_=x_rows[z, :, :, cols])
+                for h in range(2):
+                    raw[c, z, h] = t[:, h::2, :]
+
+        nc.vector.memset(sab_raw[:].bitcast(I32), 0)
+        nc.vector.memset(sq_raw[:].bitcast(I32), 0)
+        nc.gpsimd.memset(xq_plane[:].bitcast(I32), 0)
+        load_scale_rows(nc.gpsimd, xq_plane, 0, xq_scales)
+        nc.gpsimd.dma_start(out=bias[:], in_=b.rearrange("(p r) o -> p (r o)", r=PACK))
+
+        nc.sync.dma_start(
+            out=wa_raw[:].bitcast(I32).rearrange("p (z n) -> p z n", z=2),
+            in_=wa_words.rearrange("z p n t -> p z (n t)").bitcast(I32),
+        )
+        load_scale_rows(nc.sync, sab_raw, 4, wa_scales)
+        nc.sync.dma_start(
+            out=wb_raw[:].bitcast(I32).rearrange("p (z n) -> p z n", z=2),
+            in_=wb_words.rearrange("z p n -> p z n").bitcast(I32),
+        )
+        load_x(0, 0)
+        load_scale_rows(nc.sync, sab_raw, 0, wb_scales)
+        nc.sync.dma_start(out=wq_raw[:].bitcast(I32), in_=wq_words[0].bitcast(I32))
+        nc.sync.dma_start(out=xq[:].bitcast(I32), in_=xq_words[0].rearrange("p n t -> p (n t)").bitcast(I32))
+        load_x(0, 1)
+        load_scale_rows(nc.sync, sq_raw, 0, wq_scales)
+        for c in range(1, CHUNKS):
+            for z in range(2):
+                load_x(c, z)
+
+        grouped, codes, planes = {}, {}, {}
+
+        def interleave(engine_copy, dst, src):
+            engine_copy(
+                out=dst.rearrange("p (c i j) -> p c j i", i=4, j=PACK),
+                in_=src.rearrange("p j (c i) -> p c j i", i=4),
+            )
+
+        def scalar_copy(out, in_):
+            nc.scalar.activation(out=out, in_=in_, func=ACT.Copy)
+
+        def cast(c, z, h, engine_copy):
+            t = tile("x_bf%d_%d_%d" % (c, z, h), PACK * W, BF16)
+            grouped[c, z, h] = t
+            interleave(engine_copy, t[:], raw[c, z, h])
+
+        def quantize(c, z, h):
+            codes[c, z, h] = tile("x_codes%d_%d_%d" % (c, z, h), W, U32)
+            planes[c, z, h] = tile("x_plane%d_%d_%d" % (c, z, h), W, U8)
+            nc.vector.quantize_mx(
+                out=codes[c, z, h][:].bitcast(FP8X4), scales=planes[c, z, h][:], in_=grouped[c, z, h][:]
+            )
+
+        acc = {}
+        for c in range(LAST):
+            bank = ps.tile([P, PACK * W], F32, name="bank%d" % c)
+            for r in range(PACK):
+                acc[c, r] = bank[:, r * W : (r + 1) * W]
+        for r in range(PACK):
+            bank = ps.tile([P, W], F32, name="bank_last%d" % r)
+            acc[LAST, r] = bank[:]
+
+        def one_pass(c, weights, rhs, rhs_scale, first, last):
+            for r in range(PACK):
+                lhsT, lhsT_scale = weights(r)
+                nc.tensor.matmul_mx(
+                    out=acc[c, r],
+                    lhsT=lhsT,
+                    lhsT_scale=lhsT_scale,
+                    rhs=rhs,
+                    rhs_scale=rhs_scale,
+                    start=first and (r == 0 or c == LAST),
+                    stop=last and (r == PACK - 1 or c == LAST),
+                )
+
+        def x_pass(c, z, h, first=False, last=False):
+            def weights(r):
+                n0 = z * N + r * P
+                if h == 0:
+                    return wa[:, n0 : n0 + P].bitcast(FP8X4), sab[4:, n0 : n0 + P]
+                return wb[:, 2 * n0 : 2 * (n0 + P)].bitcast(FP4X4), sab[:, n0 : n0 + P]
+
+            one_pass(c, weights, codes[c, z, h][:].bitcast(FP8X4), planes[c, z, h][:], first, last)
+
+        def xq_pass(c):
+            def weights(r):
+                return wq[:, 2 * r * P : 2 * (r + 1) * P].bitcast(FP4X4), sq[:, r * P : (r + 1) * P]
+
+            cols = slice(c * W, (c + 1) * W)
+            one_pass(c, weights, xq[:, cols].bitcast(FP8X4), xq_plane[:, cols], False, False)
+
+        def tanh(c):
+            for r in range(PACK):
+                nc.scalar.activation(
+                    out=y[:, r, c * W : (c + 1) * W], in_=acc[c, r], func=ACT.Tanh, bias=bias[:, r : r + 1], scale=0.5
+                )
+
+        y_bf = {}
+
+        def round_result(c):
+            y_bf[c] = tile("y_bf%d" % c, PACK * W, BF16)
+            interleave(nc.vector.tensor_copy, y_bf[c][:], y[:, :, c * W : (c + 1) * W])
+
+        def quantize_result(c):
+            cols = slice(c * W, (c + 1) * W)
+            nc.vector.quantize_mx(out=y_codes[:, cols].bitcast(FP8X4), scales=y_plane[:, cols], in_=y_bf[c][:])
+
+        for z in range(2):
+            deal(nc, wa[:, z * N : (z + 1) * N].bitcast(I32), wa_raw[:, z * N : (z + 1) * N].bitcast(I32), 1, 4)
+        for z in range(2):
+            deal(nc, wb[:, 2 * z * N : 2 * (z + 1) * N], wb_raw[:, 2 * z * N : 2 * (z + 1) * N], 2, 1)
+        for z in range(2):
+            deal(nc, sab[:, z * N : (z + 1) * N], sab_raw[:, z * N : (z + 1) * N], 1, 1)
+        deal(nc, wq[:], wq_raw[:], 2, 1)
+
+        for c in range(CHUNKS):
+            cast(c, 0, 0, scalar_copy)
+            cast(c, 0, 1, scalar_copy if c == 0 else nc.vector.tensor_copy)
+            first, second = (0, 1) if c == 0 else (1, 0)
+            quantize(c, 0, first)
+            quantize(c, 0, second)
+            x_pass(c, 0, first, first=True)
+            x_pass(c, 0, second)
+            if 0 < c < LAST:
+                tanh(c - 1)
+            cast(c, 1, 0, scalar_copy)
+            if c == LAST:
+                tanh(c - 1)
+            cast(c, 1, 1, nc.vector.tensor_copy)
+            if c == 0:
+                deal(nc, sq[:], sq_raw[:], 1, 1)
+            xq_pass(c)
+            if 0 < c < LAST:
+                round_result(c - 1)
+            first, second = (0, 1) if c == LAST else (1, 0)
+            quantize(c, 1, first)
+            quantize(c, 1, second)
+            if c == LAST:
+                round_result(c - 1)
+            if c > 0:
+                quantize_result(c - 1)
+            x_pass(c, 1, first)
+            x_pass(c, 1, second, last=True)
+        tanh(LAST)
+        round_result(LAST)
+        quantize_result(LAST)
+
+        out_rows = out_0.rearrange("(p r) i -> p r i", r=PACK)
+        out_words = out_1[0].rearrange("p c t -> p (c t)").bitcast(I32)
+        for c0, count in STORES:
+            cols = slice(c0 * W, (c0 + count) * W)
+            nc.sync.dma_start(out=out_rows[:, :, cols], in_=y[:, :, cols])
+            nc.sync.dma_start(out=out_words[:, cols], in_=y_codes[:, cols].bitcast(I32))
+        for q in range(4):
+            queue = nc.sync if q % 2 == 0 else nc.scalar
+            queue.dma_start(
+                out=out_2[0, 4 * q : 4 * q + 4, :].bitcast(I32), in_=y_plane[32 * q : 32 * q + 4, :].bitcast(I32)
+            )

@@ -17,10 +17,9 @@ ACT = mybir.ActivationFunctionType
 P = 128
 PACK = 4
 W = 128
-CHUNKS = I // W
-LAST = CHUNKS - 1
+EARLY = [0, 1, 2]
+LATE = [3]
 LINE = 16
-STORES = [(0, 2), (2, 1), (3, 1)]
 
 
 def deal(nc, dst, src, elems, elem_bytes):
@@ -31,11 +30,11 @@ def deal(nc, dst, src, elems, elem_bytes):
     )
 
 
-def load_scale_rows(queue, plane, first, scales):
+def load_scale_rows(nc, plane, first, scales):
     passes = scales.shape[0]
     for q in range(4):
         rows = slice(32 * q + first, 32 * q + first + 4)
-        queue.dma_start(
+        nc.sync.dma_start(
             out=plane[rows, :].bitcast(I32).rearrange("r (z c) -> r z c", z=passes),
             in_=scales[:, 4 * q : 4 * q + 4, :].rearrange("z r c -> r z c").bitcast(I32),
         )
@@ -56,8 +55,8 @@ def tile_mix_halves_in_one_sum_pl_kernel(
         wa_raw, wa = tile("wa_raw", 2 * N, U32), tile("wa", 2 * N, U32)
         wb_raw, wb = tile("wb_raw", 4 * N, U8), tile("wb", 4 * N, U8)
         wq_raw, wq = tile("wq_raw", 2 * N, U8), tile("wq", 2 * N, U8)
-        sab_raw, sab = tile("sab_raw", 2 * N, U8), tile("sab", 2 * N, U8)
-        sq_raw, sq = tile("sq_raw", N, U8), tile("sq", N, U8)
+        sqa_raw, sqa = tile("sqa_raw", N, U8), tile("sqa", N, U8)
+        sb_raw, sbp = tile("sb_raw", 2 * N, U8), tile("sbp", 2 * N, U8)
         xq = tile("xq", I, U32)
         xq_plane = tile("xq_plane", I, U8)
         bias = tile("bias", PACK, F32)
@@ -65,46 +64,47 @@ def tile_mix_halves_in_one_sum_pl_kernel(
         y_codes = tile("y_codes", I, U32)
         y_plane = tile("y_plane", I, U8)
 
-        x_rows = xf.rearrange("(z p j) t -> z p (j t)", p=P, j=PACK).rearrange("z p (g i) -> z p g i", i=I)
         raw = {}
 
-        def load_x(c, z):
-            cols = slice(c * W, (c + 1) * W)
-            if (c, z) == (LAST, 1):
-                for h in range(2):
-                    t = sb.tile([P, PACK, W], F32, name="x_raw_last%d" % h, align_bytes=64)
-                    nc.sync.dma_start(out=t[:], in_=x_rows[z, :, h::2, cols])
-                    raw[c, z, h] = t[:]
-            else:
-                t = sb.tile([P, 2 * PACK, W], F32, name="x_raw%d_%d" % (c, z), align_bytes=64)
-                nc.sync.dma_start(out=t[:], in_=x_rows[z, :, :, cols])
-                for h in range(2):
-                    raw[c, z, h] = t[:, h::2, :]
+        def load_x(h, z, units):
+            width = len(units) * W
+            c0 = h * I + units[0] * W
+            t = sb.tile([P, PACK, width], F32, name="x_raw%d_%d_%d" % (h, z, units[0]), align_bytes=64)
+            rows = xf[z * P * PACK : (z + 1) * P * PACK, c0 : c0 + width]
+            nc.sync.dma_start(out=t[:], in_=rows.rearrange("(p j) i -> p j i", j=PACK))
+            for u in units:
+                raw[h, z, u] = t[:, :, (u - units[0]) * W : (u - units[0] + 1) * W]
 
-        nc.vector.memset(sab_raw[:].bitcast(I32), 0)
-        nc.vector.memset(sq_raw[:].bitcast(I32), 0)
-        nc.gpsimd.memset(xq_plane[:].bitcast(I32), 0)
-        load_scale_rows(nc.gpsimd, xq_plane, 0, xq_scales)
-        nc.gpsimd.dma_start(out=bias[:], in_=b.rearrange("(p r) o -> p (r o)", r=PACK))
+        nc.vector.memset(sqa_raw[:].bitcast(I32), 0)
+        nc.vector.memset(xq_plane[:].bitcast(I32), 0)
+        nc.vector.memset(sb_raw[:].bitcast(I32), 0)
 
         nc.sync.dma_start(
             out=wa_raw[:].bitcast(I32).rearrange("p (z n) -> p z n", z=2),
             in_=wa_words.rearrange("z p n t -> p z (n t)").bitcast(I32),
         )
-        load_scale_rows(nc.sync, sab_raw, 4, wa_scales)
+        for q in range(4):
+            nc.sync.dma_start(
+                out=sqa_raw[32 * q + 4 : 32 * q + 12, :].bitcast(I32),
+                in_=wa_scales[:, 4 * q : 4 * q + 4, :].bitcast(I32),
+            )
+        load_x(0, 0, EARLY + LATE)
+        load_scale_rows(nc, sqa_raw, 0, wq_scales)
+        nc.sync.dma_start(out=wq_raw[:].bitcast(I32), in_=wq_words[0].bitcast(I32))
+        nc.sync.dma_start(out=xq[:].bitcast(I32), in_=xq_words[0].rearrange("p n t -> p (n t)").bitcast(I32))
+        load_x(0, 1, EARLY)
+        load_scale_rows(nc, xq_plane, 0, xq_scales)
         nc.sync.dma_start(
             out=wb_raw[:].bitcast(I32).rearrange("p (z n) -> p z n", z=2),
             in_=wb_words.rearrange("z p n -> p z n").bitcast(I32),
         )
-        load_x(0, 0)
-        load_scale_rows(nc.sync, sab_raw, 0, wb_scales)
-        nc.sync.dma_start(out=wq_raw[:].bitcast(I32), in_=wq_words[0].bitcast(I32))
-        nc.sync.dma_start(out=xq[:].bitcast(I32), in_=xq_words[0].rearrange("p n t -> p (n t)").bitcast(I32))
-        load_x(0, 1)
-        load_scale_rows(nc.sync, sq_raw, 0, wq_scales)
-        for c in range(1, CHUNKS):
-            for z in range(2):
-                load_x(c, z)
+        nc.sync.dma_start(out=bias[:], in_=b.rearrange("(p r) o -> p (r o)", r=PACK))
+        load_x(1, 0, EARLY)
+        load_scale_rows(nc, sb_raw, 0, wb_scales)
+        load_x(1, 1, EARLY)
+        load_x(0, 1, LATE)
+        load_x(1, 0, LATE)
+        load_x(1, 1, LATE)
 
         grouped, codes, planes = {}, {}, {}
 
@@ -114,121 +114,139 @@ def tile_mix_halves_in_one_sum_pl_kernel(
                 in_=src.rearrange("p j (c i) -> p c j i", i=4),
             )
 
-        def scalar_copy(out, in_):
+        def on_scalar(out, in_):
             nc.scalar.activation(out=out, in_=in_, func=ACT.Copy)
 
-        def cast(c, z, h, engine_copy):
-            t = tile("x_bf%d_%d_%d" % (c, z, h), PACK * W, BF16)
-            grouped[c, z, h] = t
-            interleave(engine_copy, t[:], raw[c, z, h])
+        on_vector = nc.vector.tensor_copy
 
-        def quantize(c, z, h):
-            codes[c, z, h] = tile("x_codes%d_%d_%d" % (c, z, h), W, U32)
-            planes[c, z, h] = tile("x_plane%d_%d_%d" % (c, z, h), W, U8)
+        def cast(h, z, u, engine_copy):
+            grouped[h, z, u] = tile("x_bf%d_%d_%d" % (h, z, u), PACK * W, BF16)
+            interleave(engine_copy, grouped[h, z, u][:], raw[h, z, u])
+
+        def quantize(h, z, u):
+            codes[h, z, u] = tile("x_codes%d_%d_%d" % (h, z, u), W, U32)
+            planes[h, z, u] = tile("x_plane%d_%d_%d" % (h, z, u), W, U8)
             nc.vector.quantize_mx(
-                out=codes[c, z, h][:].bitcast(FP8X4), scales=planes[c, z, h][:], in_=grouped[c, z, h][:]
+                out=codes[h, z, u][:].bitcast(FP8X4), scales=planes[h, z, u][:], in_=grouped[h, z, u][:]
             )
 
-        acc = {}
-        for c in range(LAST):
-            bank = ps.tile([P, PACK * W], F32, name="bank%d" % c)
-            for r in range(PACK):
-                acc[c, r] = bank[:, r * W : (r + 1) * W]
+        early_banks, acc = [], {}
         for r in range(PACK):
-            bank = ps.tile([P, W], F32, name="bank_last%d" % r)
-            acc[LAST, r] = bank[:]
+            early = ps.tile([P, len(EARLY) * W], F32, name="early%d" % r)
+            late = ps.tile([P, W], F32, name="late%d" % r)
+            early_banks.append(early)
+            for u in EARLY:
+                acc[u, r] = early[:, u * W : (u + 1) * W]
+            acc[LATE[0], r] = late[:]
 
-        def one_pass(c, weights, rhs, rhs_scale, first, last):
+        def one_pass(u, weights, rhs, rhs_scale, start, stop):
             for r in range(PACK):
                 lhsT, lhsT_scale = weights(r)
                 nc.tensor.matmul_mx(
-                    out=acc[c, r],
-                    lhsT=lhsT,
-                    lhsT_scale=lhsT_scale,
-                    rhs=rhs,
-                    rhs_scale=rhs_scale,
-                    start=first and (r == 0 or c == LAST),
-                    stop=last and (r == PACK - 1 or c == LAST),
+                    out=acc[u, r], lhsT=lhsT, lhsT_scale=lhsT_scale, rhs=rhs, rhs_scale=rhs_scale, start=start, stop=stop
                 )
 
-        def x_pass(c, z, h, first=False, last=False):
+        def x_pass(h, z, u, start=False, stop=False):
             def weights(r):
                 n0 = z * N + r * P
                 if h == 0:
-                    return wa[:, n0 : n0 + P].bitcast(FP8X4), sab[4:, n0 : n0 + P]
-                return wb[:, 2 * n0 : 2 * (n0 + P)].bitcast(FP4X4), sab[:, n0 : n0 + P]
+                    return wa[:, n0 : n0 + P].bitcast(FP8X4), sqa[4 + 4 * z :, r * P : (r + 1) * P]
+                return wb[:, 2 * n0 : 2 * (n0 + P)].bitcast(FP4X4), sbp[:, n0 : n0 + P]
 
-            one_pass(c, weights, codes[c, z, h][:].bitcast(FP8X4), planes[c, z, h][:], first, last)
+            one_pass(u, weights, codes[h, z, u][:].bitcast(FP8X4), planes[h, z, u][:], start, stop)
 
-        def xq_pass(c):
+        def xq_pass(u):
             def weights(r):
-                return wq[:, 2 * r * P : 2 * (r + 1) * P].bitcast(FP4X4), sq[:, r * P : (r + 1) * P]
+                return wq[:, 2 * r * P : 2 * (r + 1) * P].bitcast(FP4X4), sqa[:, r * P : (r + 1) * P]
 
-            cols = slice(c * W, (c + 1) * W)
-            one_pass(c, weights, xq[:, cols].bitcast(FP8X4), xq_plane[:, cols], False, False)
+            cols = slice(u * W, (u + 1) * W)
+            one_pass(u, weights, xq[:, cols].bitcast(FP8X4), xq_plane[:, cols], False, False)
 
-        def tanh(c):
-            for r in range(PACK):
-                nc.scalar.activation(
-                    out=y[:, r, c * W : (c + 1) * W], in_=acc[c, r], func=ACT.Tanh, bias=bias[:, r : r + 1], scale=0.5
-                )
+        def tanh(r, cols, sums):
+            nc.scalar.activation(out=y[:, r, cols], in_=sums, func=ACT.Tanh, bias=bias[:, r : r + 1], scale=0.5)
 
         y_bf = {}
 
-        def round_result(c):
-            y_bf[c] = tile("y_bf%d" % c, PACK * W, BF16)
-            interleave(nc.vector.tensor_copy, y_bf[c][:], y[:, :, c * W : (c + 1) * W])
+        def round_result(u):
+            y_bf[u] = tile("y_bf%d" % u, PACK * W, BF16)
+            interleave(on_vector, y_bf[u][:], y[:, :, u * W : (u + 1) * W])
 
-        def quantize_result(c):
-            cols = slice(c * W, (c + 1) * W)
-            nc.vector.quantize_mx(out=y_codes[:, cols].bitcast(FP8X4), scales=y_plane[:, cols], in_=y_bf[c][:])
+        def quantize_result(u):
+            cols = slice(u * W, (u + 1) * W)
+            nc.vector.quantize_mx(out=y_codes[:, cols].bitcast(FP8X4), scales=y_plane[:, cols], in_=y_bf[u][:])
+
+        def deal_wb(z):
+            deal(nc, wb[:, 2 * z * N : 2 * (z + 1) * N], wb_raw[:, 2 * z * N : 2 * (z + 1) * N], 2, 1)
+
+        def deal_sb(z):
+            deal(nc, sbp[:, z * N : (z + 1) * N], sb_raw[:, z * N : (z + 1) * N], 1, 1)
 
         for z in range(2):
             deal(nc, wa[:, z * N : (z + 1) * N].bitcast(I32), wa_raw[:, z * N : (z + 1) * N].bitcast(I32), 1, 4)
-        for z in range(2):
-            deal(nc, wb[:, 2 * z * N : 2 * (z + 1) * N], wb_raw[:, 2 * z * N : 2 * (z + 1) * N], 2, 1)
-        for z in range(2):
-            deal(nc, sab[:, z * N : (z + 1) * N], sab_raw[:, z * N : (z + 1) * N], 1, 1)
-        deal(nc, wq[:], wq_raw[:], 2, 1)
 
-        for c in range(CHUNKS):
-            cast(c, 0, 0, scalar_copy)
-            cast(c, 0, 1, scalar_copy if c == 0 else nc.vector.tensor_copy)
-            first, second = (0, 1) if c == 0 else (1, 0)
-            quantize(c, 0, first)
-            quantize(c, 0, second)
-            x_pass(c, 0, first, first=True)
-            x_pass(c, 0, second)
-            if 0 < c < LAST:
-                tanh(c - 1)
-            cast(c, 1, 0, scalar_copy)
-            if c == LAST:
-                tanh(c - 1)
-            cast(c, 1, 1, nc.vector.tensor_copy)
-            if c == 0:
-                deal(nc, sq[:], sq_raw[:], 1, 1)
-            xq_pass(c)
-            if 0 < c < LAST:
-                round_result(c - 1)
-            first, second = (0, 1) if c == LAST else (1, 0)
-            quantize(c, 1, first)
-            quantize(c, 1, second)
-            if c == LAST:
-                round_result(c - 1)
-            if c > 0:
-                quantize_result(c - 1)
-            x_pass(c, 1, first)
-            x_pass(c, 1, second, last=True)
-        tanh(LAST)
-        round_result(LAST)
-        quantize_result(LAST)
+        cast(0, 0, 0, on_scalar)
+        cast(0, 0, 1, on_scalar)
+        cast(0, 0, 2, on_vector)
+        cast(0, 0, 3, on_vector)
+        deal(nc, sqa[:], sqa_raw[:], 1, 1)
+        quantize(0, 0, 2)
+        quantize(0, 0, 3)
+        quantize(0, 0, 0)
+        deal(nc, wq[:], wq_raw[:], 2, 1)
+        quantize(0, 0, 1)
+        x_pass(0, 0, 2, start=True)
+        x_pass(0, 0, 3, start=True)
+        x_pass(0, 0, 0)
+        x_pass(0, 0, 1)
+        for u in EARLY + LATE:
+            xq_pass(u)
+
+        for h, z, dealing in ((0, 1, deal_wb), (1, 0, deal_sb)):
+            cast(h, z, 0, on_scalar)
+            cast(h, z, 1, on_scalar)
+            cast(h, z, 2, on_vector)
+            dealing(0)
+            quantize(h, z, 2)
+            quantize(h, z, 0)
+            dealing(1)
+            quantize(h, z, 1)
+            for u in (2, 0, 1):
+                x_pass(h, z, u)
+
+        cast(1, 1, 0, on_scalar)
+        cast(1, 1, 1, on_vector)
+        cast(1, 1, 2, on_vector)
+        for u in (1, 0, 2):
+            quantize(1, 1, u)
+            x_pass(1, 1, u, stop=(u == 2))
 
         out_rows = out_0.rearrange("(p r) i -> p r i", r=PACK)
         out_words = out_1[0].rearrange("p c t -> p (c t)").bitcast(I32)
-        for c0, count in STORES:
-            cols = slice(c0 * W, (c0 + count) * W)
-            nc.sync.dma_start(out=out_rows[:, :, cols], in_=y[:, :, cols])
-            nc.sync.dma_start(out=out_words[:, cols], in_=y_codes[:, cols].bitcast(I32))
+        early_cols = slice(0, len(EARLY) * W)
+        late_cols = slice(len(EARLY) * W, I)
+        for r in range(PACK):
+            tanh(r, early_cols, early_banks[r][:])
+            nc.sync.dma_start(out=out_rows[:, r, early_cols], in_=y[:, r, early_cols])
+
+        u = LATE[0]
+        for h, z in ((0, 1), (1, 0), (1, 1)):
+            cast(h, z, u, on_vector)
+            quantize(h, z, u)
+            x_pass(h, z, u, stop=((h, z) == (1, 1)))
+        for r in range(PACK):
+            tanh(r, late_cols, acc[u, r])
+        nc.sync.dma_start(out=out_rows[:, :, late_cols], in_=y[:, :, late_cols])
+
+        round_result(0)
+        round_result(1)
+        quantize_result(0)
+        round_result(2)
+        quantize_result(1)
+        round_result(3)
+        quantize_result(2)
+        nc.sync.dma_start(out=out_words[:, early_cols], in_=y_codes[:, early_cols].bitcast(I32))
+        quantize_result(3)
+        nc.scalar.dma_start(out=out_words[:, late_cols], in_=y_codes[:, late_cols].bitcast(I32))
         for q in range(4):
             queue = nc.sync if q % 2 == 0 else nc.scalar
             queue.dma_start(

@@ -2,7 +2,7 @@ from contextlib import ExitStack
 
 import concourse.mybir as mybir
 
-K, L, T, I, N = 1024, 512, 1024, 512, 512
+K, L, I, N = 1024, 512, 512, 512
 FLOPS = 2 * N * I * (2 * K + L)
 
 F32 = mybir.dt.float32
@@ -16,10 +16,20 @@ ACT = mybir.ActivationFunctionType
 
 P = 128
 PACK = 4
-W = 128
-EARLY = [0, 1, 2]
-LATE = [3]
+PASS = P * PACK
 LINE = 16
+WA_ROW = 4
+STEP = 128
+
+EARLY = slice(0, 384)
+LATE = slice(384, 512)
+EARLY_WIDE = slice(0, 256)
+EARLY_REST = slice(256, 384)
+THIRDS = [slice(256, 384), slice(128, 256), slice(0, 128)]
+
+
+def width(cols):
+    return cols.stop - cols.start
 
 
 def deal(nc, dst, src, elems, elem_bytes):
@@ -32,12 +42,24 @@ def deal(nc, dst, src, elems, elem_bytes):
 
 def load_scale_rows(nc, plane, first, scales):
     passes = scales.shape[0]
-    for q in range(4):
-        rows = slice(32 * q + first, 32 * q + first + 4)
+    for s in range(4):
         nc.sync.dma_start(
-            out=plane[rows, :].bitcast(I32).rearrange("r (z c) -> r z c", z=passes),
-            in_=scales[:, 4 * q : 4 * q + 4, :].rearrange("z r c -> r z c").bitcast(I32),
+            out=plane[first + s : P : 32, :].bitcast(I32).rearrange("q (z c) -> q z c", z=passes),
+            in_=scales[:, s::4, :].rearrange("z q c -> q z c").bitcast(I32),
         )
+
+
+def interleave_on_vector(nc, dst, src):
+    nc.vector.tensor_copy(
+        out=dst.rearrange("p (c i j) -> p c j i", i=4, j=PACK),
+        in_=src.rearrange("p j (c i) -> p c j i", i=4),
+    )
+
+
+def interleave_on_scalar(nc, dst, src):
+    nc.scalar.activation(
+        out=dst.rearrange("p (c j) -> p c j", j=PACK), in_=src.rearrange("p j c -> p c j"), func=ACT.Copy
+    )
 
 
 def tile_mix_halves_in_one_sum_pl_kernel(
@@ -45,210 +67,218 @@ def tile_mix_halves_in_one_sum_pl_kernel(
 ):
     nc = tc.nc
     with ExitStack() as ctx:
-        sb = ctx.enter_context(tc.tile_pool(name="sb", bufs=1))
-        ps = ctx.enter_context(tc.psum_pool(name="ps", bufs=1))
+        sbuf = ctx.enter_context(tc.tile_pool(name="sbuf", bufs=1))
+        psum = ctx.enter_context(tc.psum_pool(name="psum", bufs=1))
         ctx.enter_context(tc.manual_schedule())
 
         def tile(name, cols, dtype):
-            return sb.tile([P, cols], dtype, name=name, align_bytes=64)
+            return sbuf.tile([P, cols], dtype, name=name, align_bytes=64)
 
         wa_raw, wa = tile("wa_raw", 2 * N, U32), tile("wa", 2 * N, U32)
         wb_raw, wb = tile("wb_raw", 4 * N, U8), tile("wb", 4 * N, U8)
         wq_raw, wq = tile("wq_raw", 2 * N, U8), tile("wq", 2 * N, U8)
-        sqa_raw, sqa = tile("sqa_raw", N, U8), tile("sqa", N, U8)
-        sb_raw, sbp = tile("sb_raw", 2 * N, U8), tile("sbp", 2 * N, U8)
+        wq_plane_raw, wq_plane = tile("wq_plane_raw", N, U8), tile("wq_plane", N, U8)
+        wab_plane_raw, wab_plane = tile("wab_plane_raw", 2 * N, U8), tile("wab_plane", 2 * N, U8)
         xq = tile("xq", I, U32)
         xq_plane = tile("xq_plane", I, U8)
         bias = tile("bias", PACK, F32)
-        y = sb.tile([P, PACK, I], F32, name="y", align_bytes=64)
-        y_codes = tile("y_codes", I, U32)
+        y = sbuf.tile([P, PACK, I], F32, name="y", align_bytes=64)
+        y_words = tile("y_words", I, U32)
         y_plane = tile("y_plane", I, U8)
 
-        raw = {}
-
-        def load_x(h, z, units):
-            width = len(units) * W
-            c0 = h * I + units[0] * W
-            t = sb.tile([P, PACK, width], F32, name="x_raw%d_%d_%d" % (h, z, units[0]), align_bytes=64)
-            rows = xf[z * P * PACK : (z + 1) * P * PACK, c0 : c0 + width]
-            nc.sync.dma_start(out=t[:], in_=rows.rearrange("(p j) i -> p j i", j=PACK))
-            for u in units:
-                raw[h, z, u] = t[:, :, (u - units[0]) * W : (u - units[0] + 1) * W]
-
-        nc.vector.memset(sqa_raw[:].bitcast(I32), 0)
+        nc.vector.memset(wab_plane_raw[:].bitcast(I32), 0)
+        nc.vector.memset(wq_plane_raw[:].bitcast(I32), 0)
         nc.vector.memset(xq_plane[:].bitcast(I32), 0)
-        nc.vector.memset(sb_raw[:].bitcast(I32), 0)
 
-        nc.sync.dma_start(
-            out=wa_raw[:].bitcast(I32).rearrange("p (z n) -> p z n", z=2),
-            in_=wa_words.rearrange("z p n t -> p z (n t)").bitcast(I32),
-        )
-        for q in range(4):
-            nc.sync.dma_start(
-                out=sqa_raw[32 * q + 4 : 32 * q + 12, :].bitcast(I32),
-                in_=wa_scales[:, 4 * q : 4 * q + 4, :].bitcast(I32),
-            )
-        load_x(0, 0, EARLY + LATE)
-        load_scale_rows(nc, sqa_raw, 0, wq_scales)
-        nc.sync.dma_start(out=wq_raw[:].bitcast(I32), in_=wq_words[0].bitcast(I32))
-        nc.sync.dma_start(out=xq[:].bitcast(I32), in_=xq_words[0].rearrange("p n t -> p (n t)").bitcast(I32))
-        load_x(0, 1, EARLY)
-        load_scale_rows(nc, xq_plane, 0, xq_scales)
+        x_raw = {}
+
+        def load_x(h, z, part):
+            raw = sbuf.tile([P, PACK, width(part)], F32, name="x_raw%d%d_%d" % (h, z, part.start), align_bytes=64)
+            rows = xf[z * PASS : (z + 1) * PASS, h * I + part.start : h * I + part.stop]
+            nc.sync.dma_start(out=raw[:], in_=rows.rearrange("(p j) i -> p j i", j=PACK))
+            x_raw[h, z, part.start] = raw
+
         nc.sync.dma_start(
             out=wb_raw[:].bitcast(I32).rearrange("p (z n) -> p z n", z=2),
             in_=wb_words.rearrange("z p n -> p z n").bitcast(I32),
         )
-        nc.sync.dma_start(out=bias[:], in_=b.rearrange("(p r) o -> p (r o)", r=PACK))
+        nc.sync.dma_start(
+            out=wa_raw[:].bitcast(I32).rearrange("p (z n) -> p z n", z=2),
+            in_=wa_words.rearrange("z p n t -> p z (n t)").bitcast(I32),
+        )
+        load_scale_rows(nc, wab_plane_raw, WA_ROW, wa_scales)
+        load_x(0, 0, EARLY)
+        load_scale_rows(nc, wab_plane_raw, 0, wb_scales)
+        load_x(0, 1, EARLY)
+        nc.sync.dma_start(out=wq_raw[:].bitcast(I32), in_=wq_words[0].bitcast(I32))
+        nc.sync.dma_start(out=xq[:].bitcast(I32), in_=xq_words[0].rearrange("p n t -> p (n t)").bitcast(I32))
+        load_scale_rows(nc, wq_plane_raw, 0, wq_scales)
         load_x(1, 0, EARLY)
-        load_scale_rows(nc, sb_raw, 0, wb_scales)
+        load_scale_rows(nc, xq_plane, 0, xq_scales)
+        nc.sync.dma_start(out=bias[:], in_=b.rearrange("(p r) o -> p (r o)", r=PACK))
         load_x(1, 1, EARLY)
-        load_x(0, 1, LATE)
-        load_x(1, 0, LATE)
-        load_x(1, 1, LATE)
+        for h in range(2):
+            for z in range(2):
+                load_x(h, z, LATE)
 
-        grouped, codes, planes = {}, {}, {}
+        x_bf, x_words, x_planes = {}, {}, {}
 
-        def interleave(engine_copy, dst, src):
-            engine_copy(
-                out=dst.rearrange("p (c i j) -> p c j i", i=4, j=PACK),
-                in_=src.rearrange("p j (c i) -> p c j i", i=4),
-            )
+        def round_x(h, z, cols, interleave):
+            part = LATE if cols == LATE else EARLY
+            rounded = tile("x_bf%d%d_%d" % (h, z, cols.start), PACK * width(cols), BF16)
+            raw = x_raw[h, z, part.start]
+            interleave(nc, rounded[:], raw[:, :, cols.start - part.start : cols.stop - part.start])
+            x_bf[h, z, cols.start] = rounded
 
-        def on_scalar(out, in_):
-            nc.scalar.activation(out=out, in_=in_, func=ACT.Copy)
+        def quantize_x(h, z, cols):
+            key = (h, z, cols.start)
+            x_words[key] = tile("x_words%d%d_%d" % key, width(cols), U32)
+            x_planes[key] = tile("x_plane%d%d_%d" % key, width(cols), U8)
+            nc.vector.quantize_mx(out=x_words[key][:].bitcast(FP8X4), scales=x_planes[key][:], in_=x_bf[key][:])
 
-        on_vector = nc.vector.tensor_copy
-
-        def cast(h, z, u, engine_copy):
-            grouped[h, z, u] = tile("x_bf%d_%d_%d" % (h, z, u), PACK * W, BF16)
-            interleave(engine_copy, grouped[h, z, u][:], raw[h, z, u])
-
-        def quantize(h, z, u):
-            codes[h, z, u] = tile("x_codes%d_%d_%d" % (h, z, u), W, U32)
-            planes[h, z, u] = tile("x_plane%d_%d_%d" % (h, z, u), W, U8)
-            nc.vector.quantize_mx(
-                out=codes[h, z, u][:].bitcast(FP8X4), scales=planes[h, z, u][:], in_=grouped[h, z, u][:]
-            )
-
-        early_banks, acc = [], {}
+        early_banks, late_banks = [], []
         for r in range(PACK):
-            early = ps.tile([P, len(EARLY) * W], F32, name="early%d" % r)
-            late = ps.tile([P, W], F32, name="late%d" % r)
-            early_banks.append(early)
-            for u in EARLY:
-                acc[u, r] = early[:, u * W : (u + 1) * W]
-            acc[LATE[0], r] = late[:]
+            early_bank = psum.tile([P, width(EARLY)], F32, name="early%d" % r)
+            late_bank = psum.tile([P, width(LATE)], F32, name="late%d" % r)
+            early_banks.append(early_bank)
+            late_banks.append(late_bank)
 
-        def one_pass(u, weights, rhs, rhs_scale, start, stop):
+        def sums(r, cols):
+            if cols == LATE:
+                return late_banks[r][:]
+            return early_banks[r][:, cols]
+
+        def wa_pass(z, cols, start=False):
+            key = (0, z, cols.start)
             for r in range(PACK):
-                lhsT, lhsT_scale = weights(r)
+                m0 = (2 * r + z) * P
                 nc.tensor.matmul_mx(
-                    out=acc[u, r], lhsT=lhsT, lhsT_scale=lhsT_scale, rhs=rhs, rhs_scale=rhs_scale, start=start, stop=stop
+                    out=sums(r, cols),
+                    lhsT=wa[:, m0 : m0 + P].bitcast(FP8X4),
+                    lhsT_scale=wab_plane[WA_ROW:, m0 : m0 + P],
+                    rhs=x_words[key][:].bitcast(FP8X4),
+                    rhs_scale=x_planes[key][:],
+                    start=start,
+                    stop=False,
                 )
 
-        def x_pass(h, z, u, start=False, stop=False):
-            def weights(r):
-                n0 = z * N + r * P
-                if h == 0:
-                    return wa[:, n0 : n0 + P].bitcast(FP8X4), sqa[4 + 4 * z :, r * P : (r + 1) * P]
-                return wb[:, 2 * n0 : 2 * (n0 + P)].bitcast(FP4X4), sbp[:, n0 : n0 + P]
+        def wb_matmul(z, r, cols, offset, stop=False):
+            key = (1, z, cols.start)
+            m0 = (2 * r + z) * P
+            nc.tensor.matmul_mx(
+                out=sums(r, slice(cols.start + offset, cols.start + offset + STEP)),
+                lhsT=wb[:, 2 * m0 : 2 * (m0 + P)].bitcast(FP4X4),
+                lhsT_scale=wab_plane[:, m0 : m0 + P],
+                rhs=x_words[key][:, offset : offset + STEP].bitcast(FP8X4),
+                rhs_scale=x_planes[key][:, offset : offset + STEP],
+                start=False,
+                stop=stop,
+            )
 
-            one_pass(u, weights, codes[h, z, u][:].bitcast(FP8X4), planes[h, z, u][:], start, stop)
+        def wb_pass(z, cols, stop=False):
+            for offset in range(0, width(cols), STEP):
+                for r in range(PACK):
+                    wb_matmul(z, r, cols, offset, stop)
 
-        def xq_pass(u):
-            def weights(r):
-                return wq[:, 2 * r * P : 2 * (r + 1) * P].bitcast(FP4X4), sqa[:, r * P : (r + 1) * P]
+        def wq_pass(part):
+            for c0 in range(part.start, part.stop, STEP):
+                cols = slice(c0, c0 + STEP)
+                for r in range(PACK):
+                    nc.tensor.matmul_mx(
+                        out=sums(r, cols),
+                        lhsT=wq[:, 2 * r * P : 2 * (r + 1) * P].bitcast(FP4X4),
+                        lhsT_scale=wq_plane[:, r * P : (r + 1) * P],
+                        rhs=xq[:, cols].bitcast(FP8X4),
+                        rhs_scale=xq_plane[:, cols],
+                        start=False,
+                        stop=False,
+                    )
 
-            cols = slice(u * W, (u + 1) * W)
-            one_pass(u, weights, xq[:, cols].bitcast(FP8X4), xq_plane[:, cols], False, False)
-
-        def tanh(r, cols, sums):
-            nc.scalar.activation(out=y[:, r, cols], in_=sums, func=ACT.Tanh, bias=bias[:, r : r + 1], scale=0.5)
+        def tanh_row(r, part):
+            nc.scalar.activation(
+                out=y[:, r, part], in_=sums(r, part), func=ACT.Tanh, bias=bias[:, r : r + 1], scale=0.5
+            )
 
         y_bf = {}
 
-        def round_result(u):
-            y_bf[u] = tile("y_bf%d" % u, PACK * W, BF16)
-            interleave(on_vector, y_bf[u][:], y[:, :, u * W : (u + 1) * W])
+        def round_y(cols):
+            y_bf[cols.start] = tile("y_bf%d" % cols.start, PACK * width(cols), BF16)
+            interleave_on_vector(nc, y_bf[cols.start][:], y[:, :, cols])
 
-        def quantize_result(u):
-            cols = slice(u * W, (u + 1) * W)
-            nc.vector.quantize_mx(out=y_codes[:, cols].bitcast(FP8X4), scales=y_plane[:, cols], in_=y_bf[u][:])
-
-        def deal_wb(z):
-            deal(nc, wb[:, 2 * z * N : 2 * (z + 1) * N], wb_raw[:, 2 * z * N : 2 * (z + 1) * N], 2, 1)
-
-        def deal_sb(z):
-            deal(nc, sbp[:, z * N : (z + 1) * N], sb_raw[:, z * N : (z + 1) * N], 1, 1)
-
-        for z in range(2):
-            deal(nc, wa[:, z * N : (z + 1) * N].bitcast(I32), wa_raw[:, z * N : (z + 1) * N].bitcast(I32), 1, 4)
-
-        cast(0, 0, 0, on_scalar)
-        cast(0, 0, 1, on_scalar)
-        cast(0, 0, 2, on_vector)
-        cast(0, 0, 3, on_vector)
-        deal(nc, sqa[:], sqa_raw[:], 1, 1)
-        quantize(0, 0, 2)
-        quantize(0, 0, 3)
-        quantize(0, 0, 0)
-        deal(nc, wq[:], wq_raw[:], 2, 1)
-        quantize(0, 0, 1)
-        x_pass(0, 0, 2, start=True)
-        x_pass(0, 0, 3, start=True)
-        x_pass(0, 0, 0)
-        x_pass(0, 0, 1)
-        for u in EARLY + LATE:
-            xq_pass(u)
-
-        for h, z, dealing in ((0, 1, deal_wb), (1, 0, deal_sb)):
-            cast(h, z, 0, on_scalar)
-            cast(h, z, 1, on_scalar)
-            cast(h, z, 2, on_vector)
-            dealing(0)
-            quantize(h, z, 2)
-            quantize(h, z, 0)
-            dealing(1)
-            quantize(h, z, 1)
-            for u in (2, 0, 1):
-                x_pass(h, z, u)
-
-        cast(1, 1, 0, on_scalar)
-        cast(1, 1, 1, on_vector)
-        cast(1, 1, 2, on_vector)
-        for u in (1, 0, 2):
-            quantize(1, 1, u)
-            x_pass(1, 1, u, stop=(u == 2))
+        def quantize_y(cols):
+            nc.vector.quantize_mx(
+                out=y_words[:, cols].bitcast(FP8X4), scales=y_plane[:, cols], in_=y_bf[cols.start][:]
+            )
 
         out_rows = out_0.rearrange("(p r) i -> p r i", r=PACK)
         out_words = out_1[0].rearrange("p c t -> p (c t)").bitcast(I32)
-        early_cols = slice(0, len(EARLY) * W)
-        late_cols = slice(len(EARLY) * W, I)
-        for r in range(PACK):
-            tanh(r, early_cols, early_banks[r][:])
-            nc.sync.dma_start(out=out_rows[:, r, early_cols], in_=y[:, r, early_cols])
 
-        u = LATE[0]
-        for h, z in ((0, 1), (1, 0), (1, 1)):
-            cast(h, z, u, on_vector)
-            quantize(h, z, u)
-            x_pass(h, z, u, stop=((h, z) == (1, 1)))
-        for r in range(PACK):
-            tanh(r, late_cols, acc[u, r])
-        nc.sync.dma_start(out=out_rows[:, :, late_cols], in_=y[:, :, late_cols])
+        deal(nc, wb[:], wb_raw[:], 2, 1)
+        deal(nc, wa[:].bitcast(I32), wa_raw[:].bitcast(I32), 1, 4)
+        round_x(0, 0, EARLY_WIDE, interleave_on_scalar)
+        deal(nc, wab_plane[:], wab_plane_raw[:], 1, 1)
+        round_x(0, 0, EARLY_REST, interleave_on_vector)
+        quantize_x(0, 0, EARLY_WIDE)
+        quantize_x(0, 0, EARLY_REST)
+        wa_pass(0, EARLY_WIDE, start=True)
+        wa_pass(0, EARLY_REST)
 
-        round_result(0)
-        round_result(1)
-        quantize_result(0)
-        round_result(2)
-        quantize_result(1)
-        round_result(3)
-        quantize_result(2)
-        nc.sync.dma_start(out=out_words[:, early_cols], in_=y_codes[:, early_cols].bitcast(I32))
-        quantize_result(3)
-        nc.scalar.dma_start(out=out_words[:, late_cols], in_=y_codes[:, late_cols].bitcast(I32))
-        for q in range(4):
-            queue = nc.sync if q % 2 == 0 else nc.scalar
-            queue.dma_start(
-                out=out_2[0, 4 * q : 4 * q + 4, :].bitcast(I32), in_=y_plane[32 * q : 32 * q + 4, :].bitcast(I32)
-            )
+        round_x(0, 1, EARLY_WIDE, interleave_on_scalar)
+        round_x(0, 1, EARLY_REST, interleave_on_vector)
+        deal(nc, wq[:], wq_raw[:], 2, 1)
+        quantize_x(0, 1, EARLY_REST)
+        quantize_x(0, 1, EARLY_WIDE)
+        deal(nc, wq_plane[:], wq_plane_raw[:], 1, 1)
+        wa_pass(1, EARLY_REST)
+        wa_pass(1, EARLY_WIDE)
+
+        round_x(1, 0, EARLY_WIDE, interleave_on_scalar)
+        round_x(1, 0, EARLY_REST, interleave_on_vector)
+        quantize_x(1, 0, EARLY_REST)
+        quantize_x(1, 0, EARLY_WIDE)
+        wq_pass(EARLY)
+        wb_pass(0, EARLY_REST)
+        wb_pass(0, EARLY_WIDE)
+
+        round_x(1, 1, THIRDS[1], interleave_on_scalar)
+        round_x(1, 1, THIRDS[0], interleave_on_vector)
+        round_x(1, 1, THIRDS[2], interleave_on_vector)
+        for cols in THIRDS:
+            quantize_x(1, 1, cols)
+        for r in range(PACK):
+            for cols in THIRDS:
+                wb_matmul(1, r, cols, 0, stop=(cols == THIRDS[-1]))
+
+        round_x(0, 0, LATE, interleave_on_scalar)
+        for r in range(PACK):
+            tanh_row(r, EARLY)
+            nc.sync.dma_start(out=out_rows[:, r, EARLY], in_=y[:, r, EARLY])
+
+        round_x(0, 1, LATE, interleave_on_vector)
+        quantize_x(0, 0, LATE)
+        wa_pass(0, LATE, start=True)
+        wq_pass(LATE)
+        round_x(1, 0, LATE, interleave_on_vector)
+        quantize_x(0, 1, LATE)
+        wa_pass(1, LATE)
+        quantize_x(1, 0, LATE)
+        wb_pass(0, LATE)
+        round_x(1, 1, LATE, interleave_on_vector)
+        quantize_x(1, 1, LATE)
+        wb_pass(1, LATE, stop=True)
+        for r0 in (0, 2):
+            tanh_row(r0, LATE)
+            tanh_row(r0 + 1, LATE)
+            nc.sync.dma_start(out=out_rows[:, r0 : r0 + 2, LATE], in_=y[:, r0 : r0 + 2, LATE])
+
+        round_y(EARLY_WIDE)
+        round_y(EARLY_REST)
+        quantize_y(EARLY_WIDE)
+        quantize_y(EARLY_REST)
+        nc.sync.dma_start(out=out_words[:, EARLY], in_=y_words[:, EARLY].bitcast(I32))
+        round_y(LATE)
+        quantize_y(LATE)
+        nc.scalar.dma_start(out=out_words[:, LATE], in_=y_words[:, LATE].bitcast(I32))
+        for s in range(4):
+            queue = nc.sync if s % 2 == 0 else nc.scalar
+            queue.dma_start(out=out_2[0, s::4, :].bitcast(I32), in_=y_plane[s:P:32, :].bitcast(I32))

from contextlib import ExitStack

import concourse.mybir as mybir

K, L, I, N = 1024, 512, 512, 512
FLOPS = 2 * N * I * (2 * K + L)

F32 = mybir.dt.float32
BF16 = mybir.dt.bfloat16
I32 = mybir.dt.int32
U32 = mybir.dt.uint32
U8 = mybir.dt.uint8
FP8X4 = mybir.dt.float8_e4m3fn_x4
FP4X4 = mybir.dt.float4_e2m1fn_x4
ACT = mybir.ActivationFunctionType

P = 128
PACK = 4
PASS = P * PACK
LINE = 16
WA_ROW = 4
STEP = 128

EARLY = slice(0, 384)
LATE = slice(384, 512)
EARLY_WIDE = slice(0, 256)
EARLY_REST = slice(256, 384)
THIRDS = [slice(256, 384), slice(128, 256), slice(0, 128)]


def width(cols):
    return cols.stop - cols.start


def deal(nc, dst, src, elems, elem_bytes):
    run = LINE // (elems * elem_bytes)
    nc.vector.tensor_copy(
        out=dst.rearrange("p (r c i e) -> p c r i e", r=PACK, i=run, e=elems),
        in_=src.rearrange("p (c i r e) -> p c r i e", r=PACK, i=run, e=elems),
    )


def load_scale_rows(nc, plane, first, scales):
    passes = scales.shape[0]
    for s in range(4):
        nc.sync.dma_start(
            out=plane[first + s : P : 32, :].bitcast(I32).rearrange("q (z c) -> q z c", z=passes),
            in_=scales[:, s::4, :].rearrange("z q c -> q z c").bitcast(I32),
        )


def interleave_on_vector(nc, dst, src):
    nc.vector.tensor_copy(
        out=dst.rearrange("p (c i j) -> p c j i", i=4, j=PACK),
        in_=src.rearrange("p j (c i) -> p c j i", i=4),
    )


def interleave_on_scalar(nc, dst, src):
    nc.scalar.activation(
        out=dst.rearrange("p (c j) -> p c j", j=PACK), in_=src.rearrange("p j c -> p c j"), func=ACT.Copy
    )


def tile_mix_halves_in_one_sum_pl_kernel(
    tc, xf, wa_words, wa_scales, wb_words, wb_scales, xq_words, xq_scales, wq_words, wq_scales, b, out_0, out_1, out_2
):
    nc = tc.nc
    with ExitStack() as ctx:
        sbuf = ctx.enter_context(tc.tile_pool(name="sbuf", bufs=1))
        psum = ctx.enter_context(tc.psum_pool(name="psum", bufs=1))
        ctx.enter_context(tc.manual_schedule())

        def tile(name, cols, dtype):
            return sbuf.tile([P, cols], dtype, name=name, align_bytes=64)

        wa_raw, wa = tile("wa_raw", 2 * N, U32), tile("wa", 2 * N, U32)
        wb_raw, wb = tile("wb_raw", 4 * N, U8), tile("wb", 4 * N, U8)
        wq_raw, wq = tile("wq_raw", 2 * N, U8), tile("wq", 2 * N, U8)
        wq_plane_raw, wq_plane = tile("wq_plane_raw", N, U8), tile("wq_plane", N, U8)
        wab_plane_raw, wab_plane = tile("wab_plane_raw", 2 * N, U8), tile("wab_plane", 2 * N, U8)
        xq = tile("xq", I, U32)
        xq_plane = tile("xq_plane", I, U8)
        bias = tile("bias", PACK, F32)
        y = sbuf.tile([P, PACK, I], F32, name="y", align_bytes=64)
        y_words = tile("y_words", I, U32)
        y_plane = tile("y_plane", I, U8)

        nc.vector.memset(wab_plane_raw[:].bitcast(I32), 0)
        nc.vector.memset(wq_plane_raw[:].bitcast(I32), 0)
        nc.vector.memset(xq_plane[:].bitcast(I32), 0)

        x_raw = {}

        def load_x(h, z, part):
            raw = sbuf.tile([P, PACK, width(part)], F32, name="x_raw%d%d_%d" % (h, z, part.start), align_bytes=64)
            rows = xf[z * PASS : (z + 1) * PASS, h * I + part.start : h * I + part.stop]
            nc.sync.dma_start(out=raw[:], in_=rows.rearrange("(p j) i -> p j i", j=PACK))
            x_raw[h, z, part.start] = raw

        nc.sync.dma_start(
            out=wb_raw[:].bitcast(I32).rearrange("p (z n) -> p z n", z=2),
            in_=wb_words.rearrange("z p n -> p z n").bitcast(I32),
        )
        nc.sync.dma_start(
            out=wa_raw[:].bitcast(I32).rearrange("p (z n) -> p z n", z=2),
            in_=wa_words.rearrange("z p n t -> p z (n t)").bitcast(I32),
        )
        load_scale_rows(nc, wab_plane_raw, WA_ROW, wa_scales)
        load_x(0, 0, EARLY)
        load_scale_rows(nc, wab_plane_raw, 0, wb_scales)
        load_x(0, 1, EARLY)
        nc.sync.dma_start(out=wq_raw[:].bitcast(I32), in_=wq_words[0].bitcast(I32))
        nc.sync.dma_start(out=xq[:].bitcast(I32), in_=xq_words[0].rearrange("p n t -> p (n t)").bitcast(I32))
        load_scale_rows(nc, wq_plane_raw, 0, wq_scales)
        load_x(1, 0, EARLY)
        load_scale_rows(nc, xq_plane, 0, xq_scales)
        nc.sync.dma_start(out=bias[:], in_=b.rearrange("(p r) o -> p (r o)", r=PACK))
        load_x(1, 1, EARLY)
        for h in range(2):
            for z in range(2):
                load_x(h, z, LATE)

        x_bf, x_words, x_planes = {}, {}, {}

        def round_x(h, z, cols, interleave):
            part = LATE if cols == LATE else EARLY
            rounded = tile("x_bf%d%d_%d" % (h, z, cols.start), PACK * width(cols), BF16)
            raw = x_raw[h, z, part.start]
            interleave(nc, rounded[:], raw[:, :, cols.start - part.start : cols.stop - part.start])
            x_bf[h, z, cols.start] = rounded

        def quantize_x(h, z, cols):
            key = (h, z, cols.start)
            x_words[key] = tile("x_words%d%d_%d" % key, width(cols), U32)
            x_planes[key] = tile("x_plane%d%d_%d" % key, width(cols), U8)
            nc.vector.quantize_mx(out=x_words[key][:].bitcast(FP8X4), scales=x_planes[key][:], in_=x_bf[key][:])

        early_banks, late_banks = [], []
        for r in range(PACK):
            early_bank = psum.tile([P, width(EARLY)], F32, name="early%d" % r)
            late_bank = psum.tile([P, width(LATE)], F32, name="late%d" % r)
            early_banks.append(early_bank)
            late_banks.append(late_bank)

        def sums(r, cols):
            if cols == LATE:
                return late_banks[r][:]
            return early_banks[r][:, cols]

        def wa_pass(z, cols, start=False):
            key = (0, z, cols.start)
            for r in range(PACK):
                m0 = (2 * r + z) * P
                nc.tensor.matmul_mx(
                    out=sums(r, cols),
                    lhsT=wa[:, m0 : m0 + P].bitcast(FP8X4),
                    lhsT_scale=wab_plane[WA_ROW:, m0 : m0 + P],
                    rhs=x_words[key][:].bitcast(FP8X4),
                    rhs_scale=x_planes[key][:],
                    start=start,
                    stop=False,
                )

        def wb_matmul(z, r, cols, offset, stop=False):
            key = (1, z, cols.start)
            m0 = (2 * r + z) * P
            nc.tensor.matmul_mx(
                out=sums(r, slice(cols.start + offset, cols.start + offset + STEP)),
                lhsT=wb[:, 2 * m0 : 2 * (m0 + P)].bitcast(FP4X4),
                lhsT_scale=wab_plane[:, m0 : m0 + P],
                rhs=x_words[key][:, offset : offset + STEP].bitcast(FP8X4),
                rhs_scale=x_planes[key][:, offset : offset + STEP],
                start=False,
                stop=stop,
            )

        def wb_pass(z, cols, stop=False):
            for offset in range(0, width(cols), STEP):
                for r in range(PACK):
                    wb_matmul(z, r, cols, offset, stop)

        def wq_pass(part):
            for c0 in range(part.start, part.stop, STEP):
                cols = slice(c0, c0 + STEP)
                for r in range(PACK):
                    nc.tensor.matmul_mx(
                        out=sums(r, cols),
                        lhsT=wq[:, 2 * r * P : 2 * (r + 1) * P].bitcast(FP4X4),
                        lhsT_scale=wq_plane[:, r * P : (r + 1) * P],
                        rhs=xq[:, cols].bitcast(FP8X4),
                        rhs_scale=xq_plane[:, cols],
                        start=False,
                        stop=False,
                    )

        def tanh_row(r, part):
            nc.scalar.activation(
                out=y[:, r, part], in_=sums(r, part), func=ACT.Tanh, bias=bias[:, r : r + 1], scale=0.5
            )

        y_bf = {}

        def round_y(cols):
            y_bf[cols.start] = tile("y_bf%d" % cols.start, PACK * width(cols), BF16)
            interleave_on_vector(nc, y_bf[cols.start][:], y[:, :, cols])

        def quantize_y(cols):
            nc.vector.quantize_mx(
                out=y_words[:, cols].bitcast(FP8X4), scales=y_plane[:, cols], in_=y_bf[cols.start][:]
            )

        out_rows = out_0.rearrange("(p r) i -> p r i", r=PACK)
        out_words = out_1[0].rearrange("p c t -> p (c t)").bitcast(I32)

        deal(nc, wb[:], wb_raw[:], 2, 1)
        deal(nc, wa[:].bitcast(I32), wa_raw[:].bitcast(I32), 1, 4)
        round_x(0, 0, EARLY_WIDE, interleave_on_scalar)
        deal(nc, wab_plane[:], wab_plane_raw[:], 1, 1)
        round_x(0, 0, EARLY_REST, interleave_on_vector)
        quantize_x(0, 0, EARLY_WIDE)
        quantize_x(0, 0, EARLY_REST)
        wa_pass(0, EARLY_WIDE, start=True)
        wa_pass(0, EARLY_REST)

        round_x(0, 1, EARLY_WIDE, interleave_on_scalar)
        round_x(0, 1, EARLY_REST, interleave_on_vector)
        deal(nc, wq[:], wq_raw[:], 2, 1)
        quantize_x(0, 1, EARLY_REST)
        quantize_x(0, 1, EARLY_WIDE)
        deal(nc, wq_plane[:], wq_plane_raw[:], 1, 1)
        wa_pass(1, EARLY_REST)
        wa_pass(1, EARLY_WIDE)

        round_x(1, 0, EARLY_WIDE, interleave_on_scalar)
        round_x(1, 0, EARLY_REST, interleave_on_vector)
        quantize_x(1, 0, EARLY_REST)
        quantize_x(1, 0, EARLY_WIDE)
        wq_pass(EARLY)
        wb_pass(0, EARLY_REST)
        wb_pass(0, EARLY_WIDE)

        round_x(1, 1, THIRDS[1], interleave_on_scalar)
        round_x(1, 1, THIRDS[0], interleave_on_vector)
        round_x(1, 1, THIRDS[2], interleave_on_vector)
        for cols in THIRDS:
            quantize_x(1, 1, cols)
        for r in range(PACK):
            for cols in THIRDS:
                wb_matmul(1, r, cols, 0, stop=(cols == THIRDS[-1]))

        round_x(0, 0, LATE, interleave_on_scalar)
        for r in range(PACK):
            tanh_row(r, EARLY)
            nc.sync.dma_start(out=out_rows[:, r, EARLY], in_=y[:, r, EARLY])

        round_x(0, 1, LATE, interleave_on_vector)
        quantize_x(0, 0, LATE)
        wa_pass(0, LATE, start=True)
        wq_pass(LATE)
        round_x(1, 0, LATE, interleave_on_vector)
        quantize_x(0, 1, LATE)
        wa_pass(1, LATE)
        quantize_x(1, 0, LATE)
        wb_pass(0, LATE)
        round_x(1, 1, LATE, interleave_on_vector)
        quantize_x(1, 1, LATE)
        wb_pass(1, LATE, stop=True)
        for r0 in (0, 2):
            tanh_row(r0, LATE)
            tanh_row(r0 + 1, LATE)
            nc.sync.dma_start(out=out_rows[:, r0 : r0 + 2, LATE], in_=y[:, r0 : r0 + 2, LATE])

        round_y(EARLY_WIDE)
        round_y(EARLY_REST)
        quantize_y(EARLY_WIDE)
        quantize_y(EARLY_REST)
        nc.sync.dma_start(out=out_words[:, EARLY], in_=y_words[:, EARLY].bitcast(I32))
        round_y(LATE)
        quantize_y(LATE)
        nc.scalar.dma_start(out=out_words[:, LATE], in_=y_words[:, LATE].bitcast(I32))
        for s in range(4):
            queue = nc.sync if s % 2 == 0 else nc.scalar
            queue.dma_start(out=out_2[0, s::4, :].bitcast(I32), in_=y_plane[s:P:32, :].bitcast(I32))
